import numpy as np
import ml_dtypes


def mxq(x, axis, fmt="e4m3"):
    dtype, down = {"e4m3": (ml_dtypes.float8_e4m3fn, 7), "e5m2": (ml_dtypes.float8_e5m2, 14)}[fmt]
    v = np.moveaxis(np.asarray(x, np.float32).astype(ml_dtypes.bfloat16).astype(np.float64), axis, -1)
    blocks = v.reshape(v.shape[:-1] + (-1, 32))
    amax = np.abs(blocks).max(-1, keepdims=True)
    byte = np.maximum(np.where(amax > 0, np.frexp(amax)[1] - 1 + 127, 0) - down, 1)
    scale = np.exp2(byte - 127.0)
    codes = (blocks / scale).astype(np.float32).astype(dtype).astype(np.float64)
    return np.moveaxis((codes * scale).reshape(v.shape), -1, axis)


WIDE = False


def mx_kscale(k):
    if not WIDE:
        return np.ones(k)
    levels = np.array([10, -10, 5, -5, 0])
    if k % 512:
        return np.exp2(np.random.permutation(np.resize(levels, k // 32))).repeat(32)
    a = np.empty((k // 512, 16))
    for p in range(k // 512):
        a[p, :8] = np.random.permutation(np.resize(levels, 8))
        for g in range(8):
            far = levels[np.abs(levels - a[p, g]) >= 10]
            a[p, g + 8] = far[np.random.randint(len(far))]
    return np.exp2(a.ravel()).repeat(32)


def f64(x):
    return np.asarray(x).astype(np.float64)


def striped(idx):
    return np.tile(idx.reshape(-1, 16).T, (8, 1)).astype(np.uint16)


def unstriped(offs):
    return offs[:16].T.reshape(-1).astype(np.int64)


E2M1 = np.array([0.0, 0.5, 1.0, 1.5, 2.0, 3.0, 4.0, 6.0, -0.0, -0.5, -1.0, -1.5, -2.0, -3.0, -4.0, -6.0])


def pack_weight(w, fmt):
    k, n = w.shape
    w = f64(np.asarray(w, np.float32).astype(ml_dtypes.bfloat16)).reshape(k // 32, 32, n)
    amax = np.abs(w).max(1)
    if fmt == "e4m3":
        byte = np.frexp(amax)[1] - 1 + 127 - 7
    else:
        mant, ex = np.frexp(amax / 6.0)
        byte = np.where(mant > 0.5, ex, ex - 1) + 127
    byte = np.clip(np.where(amax > 0, byte, 1), 1, 254)
    scaled = (w * np.exp2(127.0 - byte)[:, None, :]).reshape(k, n).astype(np.float32)
    by_word = np.ascontiguousarray(scaled.reshape(k // 512, 128, 4, n).transpose(0, 1, 3, 2))
    if fmt == "e4m3":
        words = by_word.astype(ml_dtypes.float8_e4m3fn).view(np.uint8)
    else:
        c = by_word.astype(ml_dtypes.float4_e2m1fn).view(np.uint8) & 0xF
        words = (c[..., 0::2] | (c[..., 1::2] << 4)).reshape(k // 512, 128, 2 * n)
    return np.ascontiguousarray(words), np.ascontiguousarray(byte.astype(np.uint8).reshape(k // 512, 16, n))


def unpack_weight(words, scales, fmt):
    g, _, n = scales.shape
    words = np.ascontiguousarray(words).reshape(g, 128, n, -1)
    if fmt == "e4m3":
        vals = words.view(ml_dtypes.float8_e4m3fn).astype(np.float64)
    else:
        nib = np.empty((g, 128, n, 4), np.uint8)
        nib[..., 0::2] = words & 0xF
        nib[..., 1::2] = words >> 4
        vals = E2M1[nib]
    vals = vals * np.repeat(np.exp2(scales.astype(np.float64) - 127.0), 8, axis=1)[..., None]
    return vals.transpose(0, 1, 3, 2).reshape(g * 512, n)


def gelu(v):
    return 0.5 * v * (1.0 + np.tanh(np.sqrt(2.0 / np.pi) * (v + 0.044715 * v**3)))


def often(T, S):
    return np.random.permutation(T)[(T * np.random.uniform(0, 1, S) ** 4).astype(np.int64)]


K, M, H, N, T, S, P = 1024, 512, 1024, 512, 4096, 1024, 512

def setup_inputs():
    n = np.random.standard_normal
    s = mx_kscale(K)[:, None]
    s2 = mx_kscale(M)[:, None]
    u = mx_kscale(H)[:, None]
    d = {}
    d["tab_words"], d["tab_scales"] = pack_weight(n((K, T)) * s, "e4m3")
    d["tab2_words"], d["tab2_scales"] = pack_weight(n((M, T)) * s2, "e4m3")
    d["tab3_words"], d["tab3_scales"] = pack_weight(n((M, T)) * s2, "e4m3")
    d["offs"] = striped(np.random.permutation(T)[:S])
    d["offs2"] = striped(np.random.permutation(T)[:S])
    d["offs3"] = striped(np.random.permutation(T)[:S])
    d["pos1"] = striped(np.random.permutation(S)[:P])
    d["pos2"] = striped(often(S, P))
    d["pos3"] = striped(often(S, P))
    d["wa"] = (n((K, H)) / K ** 0.5 / s * u.T).astype(np.float32)
    d["wb"] = (n((M, H)) / M ** 0.5 / s2 * u.T).astype(np.float32)
    d["wd_words"], d["wd_scales"] = pack_weight(n((M, H)) / M ** 0.5 / s2 * u.T, "e2m1")
    d["cap"] = ((0.2 + 0.5 * n(H)) * u[:, 0]).astype(np.float32)
    d["w4_words"], d["w4_scales"] = pack_weight(1.4 * n((H, N)) / H ** 0.5 / u, "e2m1")
    return d

def reference(tab_words, tab_scales, tab2_words, tab2_scales, tab3_words, tab3_scales, offs, offs2, offs3, pos1, pos2, pos3, wa, wb, wd_words, wd_scales, cap, w4_words, w4_scales):
    v = unpack_weight(tab_words, tab_scales, "e4m3")[:, unstriped(offs)]
    v2 = unpack_weight(tab2_words, tab2_scales, "e4m3")[:, unstriped(offs2)]
    v3 = unpack_weight(tab3_words, tab3_scales, "e4m3")[:, unstriped(offs3)]
    a = mxq(f64(wa), 0, "e4m3").T @ v
    b = mxq(f64(wb), 0, "e4m3").T @ v2
    d = unpack_weight(wd_words, wd_scales, "e2m1").T @ v3
    top = f64(cap)[:, None]
    z = np.minimum(a[:, unstriped(pos1)], top) + np.minimum(b[:, unstriped(pos2)], top) - d[:, unstriped(pos3)]
    y = unpack_weight(w4_words, w4_scales, "e2m1").T @ mxq(z, 0, "e4m3")
    return y / (1.0 + np.abs(y))

@@ -1,0 +1,297 @@
+from contextlib import ExitStack
+
+import concourse.mybir as mybir
+from concourse.masks import make_identity
+
+K, M, H, N, T, S, PICK = 1024, 512, 1024, 512, 4096, 1024, 512
+FLOPS = 2 * (K * H * S + 2 * M * H * S + H * N * PICK)
+
+F32 = mybir.dt.float32
+BF16 = mybir.dt.bfloat16
+I32 = mybir.dt.int32
+U32 = mybir.dt.uint32
+U16 = mybir.dt.uint16
+U8 = mybir.dt.uint8
+FP8X4 = mybir.dt.float8_e4m3fn_x4
+FP4X4 = mybir.dt.float4_e2m1fn_x4
+ACT = mybir.ActivationFunctionType
+ALU = mybir.AluOpType
+
+P = 128
+BANK = 512
+SLICES = H // P
+JT = PICK // P
+
+
+def tile_list_claim_rating_features_kernel(
+    tc, tab_words, tab_scales, tab2_words, tab2_scales, tab3_words, tab3_scales,
+    offs, offs2, offs3, pos1, pos2, pos3, wa, wb, wd_words, wd_scales, cap,
+    w4_words, w4_scales, out,
+):
+    nc = tc.nc
+    with ExitStack() as ctx:
+        lists = ctx.enter_context(tc.tile_pool(name="lists", bufs=1))
+        keep = ctx.enter_context(tc.tile_pool(name="keep", bufs=1))
+        ring = ctx.enter_context(tc.tile_pool(name="ring", bufs=1))
+        psum = ctx.enter_context(tc.psum_pool(name="psum", bufs=1))
+
+        def bank(i):
+            return psum.tile([P, BANK], F32, name="bank%d" % i)
+
+        def load_list(src, name):
+            t = lists.tile([P, src.shape[1]], U16, name=name)
+            nc.sync.dma_start(t[:], src)
+            return t
+
+        def load_words(src):
+            t = ring.tile([P, T], I32, name="table_words", tag="table_words", bufs=3)
+            nc.sync.dma_start(t[:], src.rearrange("p t i -> p (t i)").bitcast(I32))
+            return t
+
+        def zeroed_plane(width, name):
+            t = keep.tile([P, width], U8, name=name, align_bytes=64)
+            nc.vector.memset(t[:].bitcast(I32), 0)
+            return t
+
+        def load_scale_rows(queue, plane, first_row, src):
+            rows = 4 * src.shape[0]
+            for q in range(4):
+                lo = 32 * q + first_row
+                queue.dma_start(
+                    plane[lo : lo + rows, :].bitcast(I32),
+                    src[:, 4 * q : 4 * q + 4, :].bitcast(I32),
+                )
+
+        def load_weight(w, g, half):
+            t = ring.tile([P, 4, BANK], F32, name="raw_weight", bufs=4)
+            rows = w[512 * g : 512 * (g + 1), BANK * half : BANK * (half + 1)]
+            nc.sync.dma_start(t[:], rows.rearrange("(p t) c -> p t c", t=4))
+            return t
+
+        cap_rows = keep.tile([P, P], F32, name="cap_rows")
+        nc.gpsimd.memset(cap_rows[:], 0.0)
+        warm = keep.tile([P, 2], F32, name="warm")
+        nc.gpsimd.memset(warm[:], 1.0)
+        ident = keep.tile([P, P], F32, name="ident")
+        make_identity(nc, ident[:])
+        nc.scalar.activation(warm[:, 1:2], warm[:, 0:1], ACT.Abs_reciprocal_sqrt)
+
+        plane2 = zeroed_plane(T, "plane2")
+        plane1 = zeroed_plane(T, "plane1")
+        plane3 = zeroed_plane(T, "plane3")
+        wd_plane = zeroed_plane(H, "wd_plane")
+        w4_plane = zeroed_plane(2 * N, "w4_plane")
+
+        nc.sync.dma_start(cap_rows[0:SLICES, :], cap.rearrange("(s p) -> s p", p=P))
+        raw_b = [load_weight(wb, 0, 0)]
+        load_scale_rows(nc.sync, plane2, 4, tab2_scales)
+        idx2 = load_list(offs2, "idx2")
+        words2 = load_words(tab2_words[0])
+        raw_b.append(load_weight(wb, 0, 1))
+        p2 = load_list(pos2, "p2")
+        load_scale_rows(nc.sync, plane1, 8, tab_scales)
+        idx1 = load_list(offs, "idx1")
+        words1 = [load_words(tab_words[0])]
+        raw_a = {(0, 0): load_weight(wa, 0, 0)}
+        raw_a[(1, 0)] = load_weight(wa, 1, 0)
+        words1.append(load_words(tab_words[1]))
+        p1 = load_list(pos1, "p1")
+        idx3 = load_list(offs3, "idx3")
+        load_scale_rows(nc.sync, plane3, 0, tab3_scales)
+        raw_a[(0, 1)] = load_weight(wa, 0, 1)
+        raw_a[(1, 1)] = load_weight(wa, 1, 1)
+        words3 = load_words(tab3_words[0])
+        wd_codes = keep.tile([P, 2 * H], U8, name="wd_codes", align_bytes=64)
+        nc.sync.dma_start(wd_codes[:].bitcast(I32), wd_words[0].bitcast(I32))
+        load_scale_rows(nc.sync, wd_plane, 0, wd_scales)
+        p3 = load_list(pos3, "p3")
+        w4_codes = keep.tile([P, 2, 2 * N], U8, name="w4_codes", align_bytes=64)
+        nc.sync.dma_start(w4_codes[:].bitcast(I32), w4_words.rearrange("g p c -> p g c").bitcast(I32))
+        for q in range(4):
+            nc.sync.dma_start(
+                w4_plane[32 * q : 32 * q + 4, :].bitcast(I32).rearrange("r (g c) -> r g c", g=2),
+                w4_scales[:, 4 * q : 4 * q + 4, :].bitcast(I32).rearrange("g r c -> r g c"),
+            )
+
+        cap_bank = bank(7)
+        nc.tensor.transpose(cap_bank[:, 0:P], cap_rows[:], ident[:])
+        cap_col = keep.tile([P, SLICES], F32, name="cap_col")
+        nc.vector.tensor_copy(cap_col[:], cap_bank[:, 0:SLICES])
+        minus_two_caps = keep.tile([P, SLICES], F32, name="minus_two_caps")
+        nc.vector.tensor_scalar(minus_two_caps[:], cap_bank[:, 0:SLICES], -2.0, None, ALU.mult)
+
+        def gather_scales(plane, idx, name):
+            t = keep.tile([P, S], U8, name=name, align_bytes=64)
+            nc.vector.tensor_copy(t[:], plane[:].indirect(idx[:]))
+            return t
+
+        def gather_words(words, idx, name):
+            t = keep.tile([P, S], U32, name=name, align_bytes=64)
+            for h in range(2):
+                nc.vector.tensor_copy(
+                    t[:, BANK * h : BANK * (h + 1)],
+                    words[:].bitcast(U32).indirect(idx[:, 32 * h : 32 * (h + 1)]),
+                )
+            return t
+
+        def quantize_weight(raw, copy, name):
+            grouped = ring.tile([P, BANK, 4], BF16, name="grouped", bufs=3, align_bytes=64)
+            copy(
+                grouped[:].rearrange("p (c i) t -> p c t i", i=4),
+                raw[:].rearrange("p t (c i) -> p c t i", i=4),
+            )
+            codes = keep.tile([P, BANK], U32, name=name + "_codes", align_bytes=64)
+            scales = keep.tile([P, BANK], U8, name=name + "_scales", align_bytes=64)
+            nc.vector.quantize_mx(
+                out=codes[:].bitcast(FP8X4), scales=scales[:],
+                in_=grouped[:].rearrange("p c t -> p (c t)"),
+            )
+            return codes, scales
+
+        def first_stage(s, passes, banks, func, scale, bias, pos, name, bufs):
+            window = ring.tile([P, S], F32, name="window", bufs=5)
+            for h in range(2):
+                cols = slice(BANK * h, BANK * (h + 1))
+                acc = bank(banks[h])
+                for g, (lhs, lhs_scale, rhs, rhs_scale) in enumerate(passes):
+                    nc.tensor.matmul_mx(
+                        out=acc[:], lhsT=lhs, lhsT_scale=lhs_scale,
+                        rhs=rhs[:, cols].bitcast(FP8X4), rhs_scale=rhs_scale[:, cols],
+                        start=(g == 0), stop=(g == len(passes) - 1),
+                    )
+                nc.scalar.activation(window[:, cols], acc[:], func, bias=bias[:, s : s + 1], scale=scale)
+            picked = ring.tile([P, PICK], F32, name=name, bufs=bufs)
+            nc.vector.tensor_copy(picked[:], window[:].indirect(pos[:]))
+            return picked
+
+        def add_turned(sums, terms, start, stop):
+            for jt in range(JT):
+                for i, (picked, s) in enumerate(terms):
+                    nc.tensor.matmul(
+                        sums[jt][:, P * (s % 4) : P * (s % 4 + 1)],
+                        picked[:, P * jt : P * (jt + 1)], ident[:],
+                        is_transpose=True, start=(start and i == 0), stop=stop,
+                    )
+
+        def weight_pass(q, s):
+            codes, scales = q
+            cols = slice(P * (s % 4), P * (s % 4 + 1))
+            return codes[:, cols].bitcast(FP8X4), scales[:, cols]
+
+        qb = [quantize_weight(raw_b[0], nc.scalar.copy, "wb0")]
+        v2_scales = gather_scales(plane2, idx2, "v2_scales")
+        v2 = gather_words(words2, idx2, "v2")
+        v1_scales = gather_scales(plane1, idx1, "v1_scales")
+        v1 = []
+        picked_b = []
+        for s in range(SLICES):
+            if s == 3:
+                qb.append(quantize_weight(raw_b[1], nc.scalar.copy, "wb1"))
+            if s == 4:
+                v1.append(gather_words(words1[0], idx1, "v1_0"))
+            passes = [weight_pass(qb[s // 4], s) + (v2, v2_scales[4:P, :])]
+            picked_b.append(first_stage(s, passes, ((2 * s) % 8, (2 * s + 1) % 8), ACT.Relu, -1.0,
+                                        cap_col, p2, "picked_b", SLICES))
+        sums = [bank(4 + jt) for jt in range(JT)]
+        add_turned(sums, [(picked_b[s], s) for s in range(4)], True, False)
+
+        qa = {(0, 0): quantize_weight(raw_a[(0, 0)], nc.scalar.copy, "wa00")}
+        qa[(1, 0)] = quantize_weight(raw_a[(1, 0)], nc.scalar.copy, "wa10")
+        v1.append(gather_words(words1[1], idx1, "v1_1"))
+        qa[(0, 1)] = quantize_weight(raw_a[(0, 1)], nc.scalar.copy, "wa01")
+        qa[(1, 1)] = quantize_weight(raw_a[(1, 1)], nc.scalar.copy, "wa11")
+        v3_scales = gather_scales(plane3, idx3, "v3_scales")
+        picked_a = []
+        picked_d = []
+
+        def stage_a(s, banks):
+            passes = [weight_pass(qa[(g, s // 4)], s) + (v1[g], v1_scales[8 + 4 * g : P, :]) for g in range(2)]
+            picked_a.append(first_stage(s, passes, banks, ACT.Relu, -1.0, cap_col, p1, "picked_a", SLICES))
+
+        def stage_d(s, banks):
+            passes = [(wd_codes[:, 2 * P * s : 2 * P * (s + 1)].bitcast(FP4X4), wd_plane[:, P * s : P * (s + 1)], v3, v3_scales)]
+            picked_d.append(first_stage(s, passes, banks, ACT.Identity, 1.0, minus_two_caps, p3, "picked_d", SLICES))
+
+        for s in range(6):
+            if s == 2:
+                v3 = gather_words(words3, idx3, "v3")
+            stage_a(s, ((2 * s) % 4, (2 * s + 1) % 4))
+            if s >= 2:
+                add_turned(sums, [(picked_a[s - 2], s - 2)], False, False)
+        for s in range(4):
+            stage_d(s, ((2 * s) % 4, (2 * s + 1) % 4))
+            if s >= 2:
+                add_turned(sums, [(picked_d[s - 2], s - 2)], False, False)
+
+        z_codes = [keep.tile([P, PICK], U32, name="z_codes%d" % g, align_bytes=64) for g in range(2)]
+        z_scales = [keep.tile([P, PICK], U8, name="z_scales%d" % g, align_bytes=64) for g in range(2)]
+
+        def round_sum(total, jt):
+            turned = ring.tile([P, BANK], BF16, name="turned", bufs=4, align_bytes=64)
+            dst = turned[:].rearrange("j (u p e) -> j u p e", u=2, e=2)
+            src = total[:].rearrange("j (p u e) -> j u p e", u=2, e=2)
+            if jt % 2 == 0:
+                nc.scalar.activation(dst, src, ACT.Copy, scale=-1.0)
+            else:
+                nc.vector.tensor_scalar(dst, src, -1.0, None, ALU.mult)
+            return turned
+
+        def turn_back(turned, g, jts, spare, copy):
+            back = bank(spare)
+            width = P * len(jts)
+            for i, jt in enumerate(jts):
+                for u in range(2):
+                    nc.tensor.transpose(
+                        back[:, width * u + P * i : width * u + P * (i + 1)],
+                        turned[jt][:].bitcast(F32)[:, P * u : P * (u + 1)], ident[:],
+                    )
+            woven = ring.tile([P, width, 4], BF16, name="woven", bufs=2, align_bytes=64)
+            copy(
+                woven[:].rearrange("p j t -> p (j t)").bitcast(F32).rearrange("p (j u) -> p j u", u=2),
+                back[:, 0 : 2 * width].rearrange("p (u j) -> p j u", u=2),
+            )
+            cols = slice(P * jts[0], P * jts[0] + width)
+            nc.vector.quantize_mx(
+                out=z_codes[g][:, cols].bitcast(FP8X4), scales=z_scales[g][:, cols],
+                in_=woven[:].rearrange("p j t -> p (j t)"),
+            )
+
+        stage_a(6, (0, 1))
+        add_turned(sums, [(picked_d[2], 2)], False, False)
+        add_turned(sums, [(picked_d[3], 3)], False, True)
+        turned = [round_sum(sums[jt], jt) for jt in range(JT)]
+        sums = [bank(4 + jt) for jt in range(JT)]
+        stage_a(7, (2, 0))
+        for s in range(4, SLICES):
+            stage_d(s, ((2 * s + 2) % 3, (2 * s + 3) % 3))
+        add_turned(sums, [(picked_b[s], s) for s in range(4, SLICES)] + [(picked_a[s], s) for s in range(4, 6)], True, False)
+        turn_back(turned, 0, [0, 1], 3, nc.scalar.copy)
+        turn_back(turned, 0, [2, 3], 3, nc.scalar.copy)
+        for s in range(6, SLICES):
+            add_turned(sums, [(picked_a[s], s)], False, False)
+        for s in range(4, SLICES):
+            add_turned(sums, [(picked_d[s], s)], False, s == SLICES - 1)
+
+        turned = [round_sum(sums[jt], jt) for jt in range(JT)]
+        sizes = ring.tile([P, JT, BANK], F32, name="sizes", tag="table_words", bufs=3)
+        roots = ring.tile([P, JT, BANK], F32, name="roots", tag="table_words", bufs=3)
+        parts = ring.tile([P, JT, BANK], F32, name="parts", tag="table_words", bufs=3)
+        for jt in range(JT):
+            turn_back(turned, 1, [jt], (3 + jt) % 4, nc.vector.tensor_copy if jt % 2 == 0 else nc.scalar.copy)
+            cols = slice(P * jt, P * (jt + 1))
+            y = bank(4 + jt)
+            for nt in range(N // P):
+                for g in range(2):
+                    nc.tensor.matmul_mx(
+                        out=y[:, P * nt : P * (nt + 1)],
+                        lhsT=w4_codes[:, g, 2 * P * nt : 2 * P * (nt + 1)].bitcast(FP4X4),
+                        lhsT_scale=w4_plane[:, N * g + P * nt : N * g + P * (nt + 1)],
+                        rhs=z_codes[g][:, cols].bitcast(FP8X4), rhs_scale=z_scales[g][:, cols],
+                        start=(g == 0), stop=(g == 1),
+                    )
+            nc.scalar.activation(sizes[:, jt, :], y[:], ACT.Abs)
+            nc.scalar.activation(roots[:, jt, :], sizes[:, jt, :], ACT.Abs_reciprocal_sqrt, bias=1.0)
+            nc.vector.tensor_tensor(parts[:, jt, :], y[:], roots[:, jt, :], ALU.mult)
+            result = ring.tile([P, N // P, P], F32, name="result", bufs=JT)
+            nc.vector.tensor_tensor(result[:].rearrange("p n j -> p (n j)"), parts[:, jt, :], roots[:, jt, :], ALU.mult)
+            nc.sync.dma_start(out.rearrange("(n p) j -> p n j", p=P)[:, :, cols], result[:])

@@ -1,7 +1,6 @@
 from contextlib import ExitStack
 
 import concourse.mybir as mybir
-from concourse.masks import make_identity
 
 K, M, H, N, T, S, PICK = 1024, 512, 1024, 512, 4096, 1024, 512
 FLOPS = 2 * (K * H * S + 2 * M * H * S + H * N * PICK)
@@ -43,13 +42,13 @@ def tile_list_claim_rating_features_kernel(
             nc.sync.dma_start(t[:], src)
             return t
 
-        def load_words(src):
-            t = ring.tile([P, T], I32, name="table_words", tag="table_words", bufs=3)
+        def load_words(src, tag):
+            t = ring.tile([P, T], I32, name="table_words", tag=tag)
             nc.sync.dma_start(t[:], src.rearrange("p t i -> p (t i)").bitcast(I32))
             return t
 
         def zeroed_plane(width, name):
-            t = keep.tile([P, width], U8, name=name, align_bytes=64)
+            t = ring.tile([P, width], U8, name=name, tag=name, align_bytes=64)
             nc.vector.memset(t[:].bitcast(I32), 0)
             return t
 
@@ -62,18 +61,14 @@ def tile_list_claim_rating_features_kernel(
                     src[:, 4 * q : 4 * q + 4, :].bitcast(I32),
                 )
 
-        def load_weight(w, g, half):
-            t = ring.tile([P, 4, BANK], F32, name="raw_weight", bufs=4)
+        def load_weight(w, g, half, tag):
+            t = ring.tile([P, 4, BANK], F32, name="raw_weight", tag=tag)
             rows = w[512 * g : 512 * (g + 1), BANK * half : BANK * (half + 1)]
             nc.sync.dma_start(t[:], rows.rearrange("(p t) c -> p t c", t=4))
             return t
 
-        cap_rows = keep.tile([P, P], F32, name="cap_rows")
-        nc.gpsimd.memset(cap_rows[:], 0.0)
         warm = keep.tile([P, 2], F32, name="warm")
         nc.gpsimd.memset(warm[:], 1.0)
-        ident = keep.tile([P, P], F32, name="ident")
-        make_identity(nc, ident[:])
         nc.scalar.activation(warm[:, 1:2], warm[:, 0:1], ACT.Abs_reciprocal_sqrt)
 
         plane2 = zeroed_plane(T, "plane2")
@@ -82,27 +77,107 @@ def tile_list_claim_rating_features_kernel(
         wd_plane = zeroed_plane(H, "wd_plane")
         w4_plane = zeroed_plane(2 * N, "w4_plane")
 
-        nc.sync.dma_start(cap_rows[0:SLICES, :], cap.rearrange("(s p) -> s p", p=P))
-        raw_b = [load_weight(wb, 0, 0)]
-        load_scale_rows(nc.sync, plane2, 4, tab2_scales)
+        wd_raw = keep.tile([P, 2 * H], U8, name="wd_raw", align_bytes=64)
+        nc.sync.dma_start(wd_raw[:].bitcast(I32), wd_words[0].bitcast(I32))
         idx2 = load_list(offs2, "idx2")
-        words2 = load_words(tab2_words[0])
-        raw_b.append(load_weight(wb, 0, 1))
-        p2 = load_list(pos2, "p2")
-        load_scale_rows(nc.sync, plane1, 8, tab_scales)
+        words2 = load_words(tab2_words[0], "words23")
+        load_scale_rows(nc.sync, plane2, 4, tab2_scales)
+        raw_b = [load_weight(wb, 0, 0, "raw0")]
+        cap_col = keep.tile([P, 2, 4], F32, name="cap_col")
+        nc.sync.dma_start(cap_col[:], cap.rearrange("(g p t) -> p g t", g=2, t=4))
         idx1 = load_list(offs, "idx1")
-        words1 = [load_words(tab_words[0])]
-        raw_a = {(0, 0): load_weight(wa, 0, 0)}
-        raw_a[(1, 0)] = load_weight(wa, 1, 0)
-        words1.append(load_words(tab_words[1]))
+        raw_b.append(load_weight(wb, 0, 1, "raw1"))
+        load_scale_rows(nc.sync, plane1, 8, tab_scales)
+        p2 = load_list(pos2, "p2")
+        words1 = [load_words(tab_words[0], "words10")]
+        raw_a = {(0, 0): load_weight(wa, 0, 0, "raw2")}
+        raw_a[(1, 0)] = load_weight(wa, 1, 0, "raw0")
+        words1.append(load_words(tab_words[1], "words11"))
         p1 = load_list(pos1, "p1")
         idx3 = load_list(offs3, "idx3")
         load_scale_rows(nc.sync, plane3, 0, tab3_scales)
-        raw_a[(0, 1)] = load_weight(wa, 0, 1)
-        raw_a[(1, 1)] = load_weight(wa, 1, 1)
-        words3 = load_words(tab3_words[0])
+
         wd_codes = keep.tile([P, 2 * H], U8, name="wd_codes", align_bytes=64)
-        nc.sync.dma_start(wd_codes[:].bitcast(I32), wd_words[0].bitcast(I32))
+        nc.vector.tensor_copy(
+            wd_codes[:].rearrange("p (g t m e) -> p g t m e", g=2, t=4, e=2),
+            wd_raw[:].rearrange("p (g m t e) -> p g t m e", g=2, t=4, e=2),
+        )
+        caps = cap_col[:].rearrange("p g t -> p (g t)")
+
+        def gather_scales(plane, idx, name):
+            t = keep.tile([P, S], U8, name=name, align_bytes=64)
+            nc.vector.tensor_copy(t[:], plane[:].indirect(idx[:]))
+            return t
+
+        def gather_words(words, idx, name):
+            t = keep.tile([P, S], U32, name=name, align_bytes=64)
+            nc.vector.tensor_copy(t[:], words[:].bitcast(U32).indirect(idx[:]))
+            return t
+
+        def quantize_weight(raw, copy, name):
+            grouped = ring.tile([P, BANK, 4], BF16, name="grouped", bufs=3, align_bytes=64)
+            copy(
+                grouped[:].rearrange("p (t m) j -> p m j t", t=4),
+                raw[:].rearrange("p j (m t) -> p m j t", t=4),
+            )
+            codes = keep.tile([P, BANK], U32, name=name + "_codes", align_bytes=64)
+            scales = keep.tile([P, BANK], U8, name=name + "_scales", align_bytes=64)
+            nc.vector.quantize_mx(
+                out=codes[:].bitcast(FP8X4), scales=scales[:],
+                in_=grouped[:].rearrange("p c t -> p (c t)"),
+            )
+            return codes, scales
+
+        def first_stage(first_bank, passes, func, scale, bias, tag=None):
+            if tag is None:
+                window = ring.tile([P, S], F32, name="window", bufs=8)
+            else:
+                window = ring.tile([P, S], F32, name="window", tag=tag)
+            for h in range(2):
+                cols = slice(BANK * h, BANK * (h + 1))
+                acc = bank(first_bank + h)
+                for g, (lhs, lhs_scale, rhs, rhs_scale) in enumerate(passes):
+                    nc.tensor.matmul_mx(
+                        out=acc[:], lhsT=lhs, lhsT_scale=lhs_scale,
+                        rhs=rhs[:, cols].bitcast(FP8X4), rhs_scale=rhs_scale[:, cols],
+                        start=(g == 0), stop=(g == len(passes) - 1),
+                    )
+                nc.scalar.activation(window[:, cols], acc[:], func, bias=bias, scale=scale)
+            return window
+
+        def pick(picked, window, pos):
+            nc.vector.tensor_copy(picked, window[:].indirect(pos))
+            return picked
+
+        def pick_and(op, result, window, pos, other):
+            nc.vector.tensor_tensor(result, window[:].indirect(pos), other, op)
+            return result
+
+        def weight_pass(q, s):
+            codes, scales = q
+            cols = slice(P * (s % 4), P * (s % 4 + 1))
+            return codes[:, cols].bitcast(FP8X4), scales[:, cols]
+
+        v2 = gather_words(words2, idx2, "v2")
+        v2_scales = gather_scales(plane2, idx2, "v2_scales")
+        qb = [quantize_weight(raw_b[0], nc.scalar.copy, "wb0")]
+        v1_scales = gather_scales(plane1, idx1, "v1_scales")
+        v1 = []
+        picked_b = []
+        early_b = ring.tile([P, 4, PICK], F32, name="early_b")
+        for s in range(SLICES):
+            if s == 2:
+                qb.append(quantize_weight(raw_b[1], nc.scalar.copy, "wb1"))
+            if s == 4:
+                v1.append(gather_words(words1[0], idx1, "v1_0"))
+                late_b = ring.tile([P, 4, PICK], F32, name="late_b", tag="words10")
+            passes = [weight_pass(qb[s // 4], s) + (v2, v2_scales[4:P, :])]
+            window = first_stage((2 * s) % 8, passes, ACT.Relu, -1.0, caps[:, s : s + 1], "raw1" if s == 2 else None)
+            picked_b.append(pick((early_b if s < 4 else late_b)[:, s % 4, :], window, p2[:]))
+
+        raw_a[(0, 1)] = load_weight(wa, 0, 1, "raw1")
+        raw_a[(1, 1)] = load_weight(wa, 1, 1, "raw3")
+        words3 = load_words(tab3_words[0], "words23")
         load_scale_rows(nc.sync, wd_plane, 0, wd_scales)
         p3 = load_list(pos3, "p3")
         w4_codes = keep.tile([P, 2, 2 * N], U8, name="w4_codes", align_bytes=64)
@@ -113,185 +188,94 @@ def tile_list_claim_rating_features_kernel(
                 w4_scales[:, 4 * q : 4 * q + 4, :].bitcast(I32).rearrange("g r c -> r g c"),
             )
 
-        cap_bank = bank(7)
-        nc.tensor.transpose(cap_bank[:, 0:P], cap_rows[:], ident[:])
-        cap_col = keep.tile([P, SLICES], F32, name="cap_col")
-        nc.vector.tensor_copy(cap_col[:], cap_bank[:, 0:SLICES])
-        minus_two_caps = keep.tile([P, SLICES], F32, name="minus_two_caps")
-        nc.vector.tensor_scalar(minus_two_caps[:], cap_bank[:, 0:SLICES], -2.0, None, ALU.mult)
-
-        def gather_scales(plane, idx, name):
-            t = keep.tile([P, S], U8, name=name, align_bytes=64)
-            nc.vector.tensor_copy(t[:], plane[:].indirect(idx[:]))
-            return t
-
-        def gather_words(words, idx, name):
-            t = keep.tile([P, S], U32, name=name, align_bytes=64)
-            for h in range(2):
-                nc.vector.tensor_copy(
-                    t[:, BANK * h : BANK * (h + 1)],
-                    words[:].bitcast(U32).indirect(idx[:, 32 * h : 32 * (h + 1)]),
-                )
-            return t
-
-        def quantize_weight(raw, copy, name):
-            grouped = ring.tile([P, BANK, 4], BF16, name="grouped", bufs=3, align_bytes=64)
-            copy(
-                grouped[:].rearrange("p (c i) t -> p c t i", i=4),
-                raw[:].rearrange("p t (c i) -> p c t i", i=4),
-            )
-            codes = keep.tile([P, BANK], U32, name=name + "_codes", align_bytes=64)
-            scales = keep.tile([P, BANK], U8, name=name + "_scales", align_bytes=64)
-            nc.vector.quantize_mx(
-                out=codes[:].bitcast(FP8X4), scales=scales[:],
-                in_=grouped[:].rearrange("p c t -> p (c t)"),
-            )
-            return codes, scales
-
-        def first_stage(s, passes, banks, func, scale, bias, pos, name, bufs):
-            window = ring.tile([P, S], F32, name="window", bufs=5)
-            for h in range(2):
-                cols = slice(BANK * h, BANK * (h + 1))
-                acc = bank(banks[h])
-                for g, (lhs, lhs_scale, rhs, rhs_scale) in enumerate(passes):
-                    nc.tensor.matmul_mx(
-                        out=acc[:], lhsT=lhs, lhsT_scale=lhs_scale,
-                        rhs=rhs[:, cols].bitcast(FP8X4), rhs_scale=rhs_scale[:, cols],
-                        start=(g == 0), stop=(g == len(passes) - 1),
-                    )
-                nc.scalar.activation(window[:, cols], acc[:], func, bias=bias[:, s : s + 1], scale=scale)
-            picked = ring.tile([P, PICK], F32, name=name, bufs=bufs)
-            nc.vector.tensor_copy(picked[:], window[:].indirect(pos[:]))
-            return picked
-
-        def add_turned(sums, terms, start, stop):
-            for jt in range(JT):
-                for i, (picked, s) in enumerate(terms):
-                    nc.tensor.matmul(
-                        sums[jt][:, P * (s % 4) : P * (s % 4 + 1)],
-                        picked[:, P * jt : P * (jt + 1)], ident[:],
-                        is_transpose=True, start=(start and i == 0), stop=stop,
-                    )
-
-        def weight_pass(q, s):
-            codes, scales = q
-            cols = slice(P * (s % 4), P * (s % 4 + 1))
-            return codes[:, cols].bitcast(FP8X4), scales[:, cols]
-
-        qb = [quantize_weight(raw_b[0], nc.scalar.copy, "wb0")]
-        v2_scales = gather_scales(plane2, idx2, "v2_scales")
-        v2 = gather_words(words2, idx2, "v2")
-        v1_scales = gather_scales(plane1, idx1, "v1_scales")
-        v1 = []
-        picked_b = []
-        for s in range(SLICES):
-            if s == 3:
-                qb.append(quantize_weight(raw_b[1], nc.scalar.copy, "wb1"))
-            if s == 4:
-                v1.append(gather_words(words1[0], idx1, "v1_0"))
-            passes = [weight_pass(qb[s // 4], s) + (v2, v2_scales[4:P, :])]
-            picked_b.append(first_stage(s, passes, ((2 * s) % 8, (2 * s + 1) % 8), ACT.Relu, -1.0,
-                                        cap_col, p2, "picked_b", SLICES))
-        sums = [bank(4 + jt) for jt in range(JT)]
-        add_turned(sums, [(picked_b[s], s) for s in range(4)], True, False)
-
         qa = {(0, 0): quantize_weight(raw_a[(0, 0)], nc.scalar.copy, "wa00")}
         qa[(1, 0)] = quantize_weight(raw_a[(1, 0)], nc.scalar.copy, "wa10")
         v1.append(gather_words(words1[1], idx1, "v1_1"))
         qa[(0, 1)] = quantize_weight(raw_a[(0, 1)], nc.scalar.copy, "wa01")
         qa[(1, 1)] = quantize_weight(raw_a[(1, 1)], nc.scalar.copy, "wa11")
         v3_scales = gather_scales(plane3, idx3, "v3_scales")
-        picked_a = []
-        picked_d = []
-
-        def stage_a(s, banks):
-            passes = [weight_pass(qa[(g, s // 4)], s) + (v1[g], v1_scales[8 + 4 * g : P, :]) for g in range(2)]
-            picked_a.append(first_stage(s, passes, banks, ACT.Relu, -1.0, cap_col, p1, "picked_a", SLICES))
-
-        def stage_d(s, banks):
-            passes = [(wd_codes[:, 2 * P * s : 2 * P * (s + 1)].bitcast(FP4X4), wd_plane[:, P * s : P * (s + 1)], v3, v3_scales)]
-            picked_d.append(first_stage(s, passes, banks, ACT.Identity, 1.0, minus_two_caps, p3, "picked_d", SLICES))
-
-        for s in range(6):
-            if s == 2:
+        cap_for_a = ring.tile([P, SLICES], F32, name="cap_for_a", tag="raw3")
+        nc.scalar.copy(cap_for_a[:], caps)
+        two_caps = keep.tile([P, SLICES], F32, name="two_caps")
+        nc.scalar.mul(two_caps[:], caps, 2.0)
+        wd_scale_plane = keep.tile([P, H], U8, name="wd_scale_plane", align_bytes=64)
+        nc.vector.tensor_copy(
+            wd_scale_plane[:].rearrange("p (g t m) -> p g t m", g=2, t=4),
+            wd_plane[:].rearrange("p (g m t) -> p g t m", g=2, t=4),
+        )
+        joined = []
+        early_a = ring.tile([P, 4, PICK], F32, name="early_a")
+        for s in range(SLICES):
+            if s == 4:
                 v3 = gather_words(words3, idx3, "v3")
-            stage_a(s, ((2 * s) % 4, (2 * s + 1) % 4))
-            if s >= 2:
-                add_turned(sums, [(picked_a[s - 2], s - 2)], False, False)
-        for s in range(4):
-            stage_d(s, ((2 * s) % 4, (2 * s + 1) % 4))
-            if s >= 2:
-                add_turned(sums, [(picked_d[s - 2], s - 2)], False, False)
+                late_a = ring.tile([P, 4, PICK], F32, name="late_a", tag="words23")
+            passes = [weight_pass(qa[(g, s // 4)], s) + (v1[g], v1_scales[8 + 4 * g : P, :]) for g in range(2)]
+            window = first_stage((2 * s) % 8, passes, ACT.Relu, -1.0, cap_for_a[:, s : s + 1])
+            joined.append(pick_and(ALU.add, (early_a if s < 4 else late_a)[:, s % 4, :], window, p1[:], picked_b[s]))
+
+        half = PICK // 2
+        windows_d = []
+        z_first = ring.tile([P, 4, PICK], F32, name="z_first")
+        z_left = ring.tile([P, 4, half], F32, name="z_left")
+        for s in range(SLICES):
+            passes = [(wd_codes[:, 2 * P * s : 2 * P * (s + 1)].bitcast(FP4X4), wd_scale_plane[:, P * s : P * (s + 1)], v3, v3_scales)]
+            window = first_stage((2 * s) % 8, passes, ACT.Identity, -1.0, two_caps[:, s : s + 1])
+            windows_d.append(window)
+            if s < 4:
+                pick_and(ALU.subtract, z_first[:, s, :], window, p3[:], joined[s])
+            else:
+                pick_and(ALU.subtract, z_left[:, s - 4, :], window, p3[:, 0:16], joined[s][:, 0:half])
 
         z_codes = [keep.tile([P, PICK], U32, name="z_codes%d" % g, align_bytes=64) for g in range(2)]
         z_scales = [keep.tile([P, PICK], U8, name="z_scales%d" % g, align_bytes=64) for g in range(2)]
 
-        def round_sum(total, jt):
-            turned = ring.tile([P, BANK], BF16, name="turned", bufs=4, align_bytes=64)
-            dst = turned[:].rearrange("j (u p e) -> j u p e", u=2, e=2)
-            src = total[:].rearrange("j (p u e) -> j u p e", u=2, e=2)
-            if jt % 2 == 0:
-                nc.scalar.activation(dst, src, ACT.Copy, scale=-1.0)
-            else:
-                nc.vector.tensor_scalar(dst, src, -1.0, None, ALU.mult)
-            return turned
-
-        def turn_back(turned, g, jts, spare, copy):
-            back = bank(spare)
-            width = P * len(jts)
-            for i, jt in enumerate(jts):
-                for u in range(2):
-                    nc.tensor.transpose(
-                        back[:, width * u + P * i : width * u + P * (i + 1)],
-                        turned[jt][:].bitcast(F32)[:, P * u : P * (u + 1)], ident[:],
-                    )
-            woven = ring.tile([P, width, 4], BF16, name="woven", bufs=2, align_bytes=64)
+        def quantize_z(rows, g, first, copy, tag):
+            width = rows.shape[2]
+            woven = ring.tile([P, width, 4], BF16, name="woven", tag=tag, align_bytes=64)
             copy(
-                woven[:].rearrange("p j t -> p (j t)").bitcast(F32).rearrange("p (j u) -> p j u", u=2),
-                back[:, 0 : 2 * width].rearrange("p (u j) -> p j u", u=2),
+                woven[:].rearrange("p (c i) t -> p c t i", i=4),
+                rows.rearrange("p t (c i) -> p c t i", i=4),
             )
-            cols = slice(P * jts[0], P * jts[0] + width)
+            cols = slice(first, first + width)
             nc.vector.quantize_mx(
                 out=z_codes[g][:, cols].bitcast(FP8X4), scales=z_scales[g][:, cols],
                 in_=woven[:].rearrange("p j t -> p (j t)"),
             )
 
-        stage_a(6, (0, 1))
-        add_turned(sums, [(picked_d[2], 2)], False, False)
-        add_turned(sums, [(picked_d[3], 3)], False, True)
-        turned = [round_sum(sums[jt], jt) for jt in range(JT)]
-        sums = [bank(4 + jt) for jt in range(JT)]
-        stage_a(7, (2, 0))
+        quantize_z(z_first[:, :, 0:half], 0, 0, nc.scalar.copy, "woven0")
+        z_right = ring.tile([P, 4, half], F32, name="z_right", tag="woven0", align_bytes=64)
         for s in range(4, SLICES):
-            stage_d(s, ((2 * s + 2) % 3, (2 * s + 3) % 3))
-        add_turned(sums, [(picked_b[s], s) for s in range(4, SLICES)] + [(picked_a[s], s) for s in range(4, 6)], True, False)
-        turn_back(turned, 0, [0, 1], 3, nc.scalar.copy)
-        turn_back(turned, 0, [2, 3], 3, nc.scalar.copy)
-        for s in range(6, SLICES):
-            add_turned(sums, [(picked_a[s], s)], False, False)
-        for s in range(4, SLICES):
-            add_turned(sums, [(picked_d[s], s)], False, s == SLICES - 1)
+            pick_and(ALU.subtract, z_right[:, s - 4, :], windows_d[s], p3[:, 16:32], joined[s][:, half:PICK])
+        quantize_z(z_first[:, :, half:PICK], 0, half, nc.scalar.copy, "woven1")
+        ys = [bank(jt) for jt in range(JT)]
 
-        turned = [round_sum(sums[jt], jt) for jt in range(JT)]
-        sizes = ring.tile([P, JT, BANK], F32, name="sizes", tag="table_words", bufs=3)
-        roots = ring.tile([P, JT, BANK], F32, name="roots", tag="table_words", bufs=3)
-        parts = ring.tile([P, JT, BANK], F32, name="parts", tag="table_words", bufs=3)
-        for jt in range(JT):
-            turn_back(turned, 1, [jt], (3 + jt) % 4, nc.vector.tensor_copy if jt % 2 == 0 else nc.scalar.copy)
+        def last_product(g, jt):
             cols = slice(P * jt, P * (jt + 1))
-            y = bank(4 + jt)
             for nt in range(N // P):
-                for g in range(2):
-                    nc.tensor.matmul_mx(
-                        out=y[:, P * nt : P * (nt + 1)],
-                        lhsT=w4_codes[:, g, 2 * P * nt : 2 * P * (nt + 1)].bitcast(FP4X4),
-                        lhsT_scale=w4_plane[:, N * g + P * nt : N * g + P * (nt + 1)],
-                        rhs=z_codes[g][:, cols].bitcast(FP8X4), rhs_scale=z_scales[g][:, cols],
-                        start=(g == 0), stop=(g == 1),
-                    )
+                nc.tensor.matmul_mx(
+                    out=ys[jt][:, P * nt : P * (nt + 1)],
+                    lhsT=w4_codes[:, g, 2 * P * nt : 2 * P * (nt + 1)].bitcast(FP4X4),
+                    lhsT_scale=w4_plane[:, N * g + P * nt : N * g + P * (nt + 1)],
+                    rhs=z_codes[g][:, cols].bitcast(FP8X4), rhs_scale=z_scales[g][:, cols],
+                    start=(g == 0 and nt == 0), stop=(g == 1 and nt == N // P - 1),
+                )
+
+        for jt in range(JT):
+            last_product(0, jt)
+        for jt in range(JT):
+            rows = (z_left if jt < 2 else z_right)[:, :, P * (jt % 2) : P * (jt % 2 + 1)]
+            quantize_z(rows, 1, P * jt, nc.vector.tensor_copy if jt == 3 else nc.scalar.copy, "woven_last%d" % jt)
+            last_product(1, jt)
+
+        sizes = ring.tile([P, JT, BANK], F32, name="sizes", tag="words11")
+        roots = ring.tile([P, JT, BANK], F32, name="roots", tag="raw1")
+        parts = ring.tile([P, JT, BANK], F32, name="parts", tag="raw0")
+        results = ring.tile([P, JT, BANK], F32, name="results", tag="raw2")
+        for jt in range(JT):
+            cols = slice(P * jt, P * (jt + 1))
+            y = ys[jt]
             nc.scalar.activation(sizes[:, jt, :], y[:], ACT.Abs)
             nc.scalar.activation(roots[:, jt, :], sizes[:, jt, :], ACT.Abs_reciprocal_sqrt, bias=1.0)
             nc.vector.tensor_tensor(parts[:, jt, :], y[:], roots[:, jt, :], ALU.mult)
-            result = ring.tile([P, N // P, P], F32, name="result", bufs=JT)
-            nc.vector.tensor_tensor(result[:].rearrange("p n j -> p (n j)"), parts[:, jt, :], roots[:, jt, :], ALU.mult)
-            nc.sync.dma_start(out.rearrange("(n p) j -> p n j", p=P)[:, :, cols], result[:])
+            nc.vector.tensor_tensor(results[:, jt, :], parts[:, jt, :], roots[:, jt, :], ALU.mult)
+            nc.sync.dma_start(out.rearrange("(n p) j -> p n j", p=P)[:, :, cols], results[:, jt, :].rearrange("p (n j) -> p n j", j=P))

@@ -72,36 +72,31 @@ def tile_list_claim_rating_features_kernel(
         nc.scalar.activation(warm[:, 1:2], warm[:, 0:1], ACT.Abs_reciprocal_sqrt)
 
         plane2 = zeroed_plane(T, "plane2")
-        plane1 = zeroed_plane(T, "plane1")
-        plane3 = zeroed_plane(T, "plane3")
         wd_plane = zeroed_plane(H, "wd_plane")
+        plane3 = zeroed_plane(T, "plane3")
+        plane1 = zeroed_plane(T, "plane1")
         w4_plane = zeroed_plane(2 * N, "w4_plane")
 
+        raw_b = [load_weight(wb, 0, 0, "raw0")]
+        load_scale_rows(nc.sync, plane2, 4, tab2_scales)
+        idx2 = load_list(offs2, "idx2")
         wd_raw = keep.tile([P, 2 * H], U8, name="wd_raw", align_bytes=64)
         nc.sync.dma_start(wd_raw[:].bitcast(I32), wd_words[0].bitcast(I32))
-        idx2 = load_list(offs2, "idx2")
-        words2 = load_words(tab2_words[0], "words23")
-        load_scale_rows(nc.sync, plane2, 4, tab2_scales)
-        raw_b = [load_weight(wb, 0, 0, "raw0")]
+        words2 = load_words(tab2_words[0], "words2")
         cap_col = keep.tile([P, 2, 4], F32, name="cap_col")
         nc.sync.dma_start(cap_col[:], cap.rearrange("(g p t) -> p g t", g=2, t=4))
-        idx1 = load_list(offs, "idx1")
-        raw_b.append(load_weight(wb, 0, 1, "raw1"))
-        load_scale_rows(nc.sync, plane1, 8, tab_scales)
         p2 = load_list(pos2, "p2")
-        words1 = [load_words(tab_words[0], "words10")]
-        raw_a = {(0, 0): load_weight(wa, 0, 0, "raw2")}
-        raw_a[(1, 0)] = load_weight(wa, 1, 0, "raw0")
-        words1.append(load_words(tab_words[1], "words11"))
-        p1 = load_list(pos1, "p1")
+        load_scale_rows(nc.sync, wd_plane, 0, wd_scales)
+        raw_b.append(load_weight(wb, 0, 1, "raw1"))
+        words3 = load_words(tab3_words[0], "words3")
         idx3 = load_list(offs3, "idx3")
         load_scale_rows(nc.sync, plane3, 0, tab3_scales)
-
-        wd_codes = keep.tile([P, 2 * H], U8, name="wd_codes", align_bytes=64)
-        nc.vector.tensor_copy(
-            wd_codes[:].rearrange("p (g t m e) -> p g t m e", g=2, t=4, e=2),
-            wd_raw[:].rearrange("p (g m t e) -> p g t m e", g=2, t=4, e=2),
-        )
+        p3 = load_list(pos3, "p3")
+        words1 = [load_words(tab_words[0], "words10")]
+        idx1 = load_list(offs, "idx1")
+        load_scale_rows(nc.sync, plane1, 8, tab_scales)
+        raw_a = {(0, 0): load_weight(wa, 0, 0, "raw2")}
+        raw_a[(1, 0)] = load_weight(wa, 1, 0, "raw0")
         caps = cap_col[:].rearrange("p g t -> p (g t)")
 
         def gather_scales(plane, idx, name):
@@ -109,14 +104,19 @@ def tile_list_claim_rating_features_kernel(
             nc.vector.tensor_copy(t[:], plane[:].indirect(idx[:]))
             return t
 
-        def gather_words(words, idx, name):
+        def gather_words(words, idx, name, pieces=1):
             t = keep.tile([P, S], U32, name=name, align_bytes=64)
-            nc.vector.tensor_copy(t[:], words[:].bitcast(U32).indirect(idx[:]))
+            width = S // pieces
+            for i in range(pieces):
+                nc.vector.tensor_copy(
+                    t[:, width * i : width * (i + 1)],
+                    words[:].bitcast(U32).indirect(idx[:, width // 16 * i : width // 16 * (i + 1)]),
+                )
             return t
 
-        def quantize_weight(raw, copy, name):
+        def quantize_weight(raw, name):
             grouped = ring.tile([P, BANK, 4], BF16, name="grouped", bufs=3, align_bytes=64)
-            copy(
+            nc.scalar.copy(
                 grouped[:].rearrange("p (t m) j -> p m j t", t=4),
                 raw[:].rearrange("p j (m t) -> p m j t", t=4),
             )
@@ -158,28 +158,36 @@ def tile_list_claim_rating_features_kernel(
             cols = slice(P * (s % 4), P * (s % 4 + 1))
             return codes[:, cols].bitcast(FP8X4), scales[:, cols]
 
-        v2 = gather_words(words2, idx2, "v2")
         v2_scales = gather_scales(plane2, idx2, "v2_scales")
-        qb = [quantize_weight(raw_b[0], nc.scalar.copy, "wb0")]
-        v1_scales = gather_scales(plane1, idx1, "v1_scales")
-        v1 = []
+        qb = [quantize_weight(raw_b[0], "wb0")]
+        v2 = gather_words(words2, idx2, "v2", 2)
+        wd_codes = keep.tile([P, 2 * H], U8, name="wd_codes", align_bytes=64)
+        nc.vector.tensor_copy(
+            wd_codes[:].rearrange("p (g t m e) -> p g t m e", g=2, t=4, e=2),
+            wd_raw[:].rearrange("p (g m t e) -> p g t m e", g=2, t=4, e=2),
+        )
+        wd_scale_plane = keep.tile([P, H], U8, name="wd_scale_plane", align_bytes=64)
+        nc.vector.tensor_copy(
+            wd_scale_plane[:].rearrange("p (g t m) -> p g t m", g=2, t=4),
+            wd_plane[:].rearrange("p (g m t) -> p g t m", g=2, t=4),
+        )
         picked_b = []
         early_b = ring.tile([P, 4, PICK], F32, name="early_b")
         for s in range(SLICES):
             if s == 2:
-                qb.append(quantize_weight(raw_b[1], nc.scalar.copy, "wb1"))
+                qb.append(quantize_weight(raw_b[1], "wb1"))
             if s == 4:
-                v1.append(gather_words(words1[0], idx1, "v1_0"))
-                late_b = ring.tile([P, 4, PICK], F32, name="late_b", tag="words10")
+                v3 = gather_words(words3, idx3, "v3")
+                v3_scales = gather_scales(plane3, idx3, "v3_scales")
+                late_b = ring.tile([P, 4, PICK], F32, name="late_b", tag="plane3", align_bytes=64)
             passes = [weight_pass(qb[s // 4], s) + (v2, v2_scales[4:P, :])]
             window = first_stage((2 * s) % 8, passes, ACT.Relu, -1.0, caps[:, s : s + 1], "raw1" if s == 2 else None)
             picked_b.append(pick((early_b if s < 4 else late_b)[:, s % 4, :], window, p2[:]))
 
+        words1.append(load_words(tab_words[1], "words2"))
+        p1 = load_list(pos1, "p1")
         raw_a[(0, 1)] = load_weight(wa, 0, 1, "raw1")
         raw_a[(1, 1)] = load_weight(wa, 1, 1, "raw3")
-        words3 = load_words(tab3_words[0], "words23")
-        load_scale_rows(nc.sync, wd_plane, 0, wd_scales)
-        p3 = load_list(pos3, "p3")
         w4_codes = keep.tile([P, 2, 2 * N], U8, name="w4_codes", align_bytes=64)
         nc.sync.dma_start(w4_codes[:].bitcast(I32), w4_words.rearrange("g p c -> p g c").bitcast(I32))
         for q in range(4):
@@ -188,65 +196,66 @@ def tile_list_claim_rating_features_kernel(
                 w4_scales[:, 4 * q : 4 * q + 4, :].bitcast(I32).rearrange("g r c -> r g c"),
             )
 
-        qa = {(0, 0): quantize_weight(raw_a[(0, 0)], nc.scalar.copy, "wa00")}
-        qa[(1, 0)] = quantize_weight(raw_a[(1, 0)], nc.scalar.copy, "wa10")
-        v1.append(gather_words(words1[1], idx1, "v1_1"))
-        qa[(0, 1)] = quantize_weight(raw_a[(0, 1)], nc.scalar.copy, "wa01")
-        qa[(1, 1)] = quantize_weight(raw_a[(1, 1)], nc.scalar.copy, "wa11")
-        v3_scales = gather_scales(plane3, idx3, "v3_scales")
+        joined = []
+        qa = {}
+        v1 = []
+        for s in range(SLICES):
+            if s == 0:
+                two_caps = keep.tile([P, 4], F32, name="two_caps")
+                nc.scalar.mul(two_caps[:], caps[:, 0:4], 2.0)
+                joined_tile = ring.tile([P, 2, PICK], F32, name="joined01")
+            if s == 2:
+                v1.append(gather_words(words1[0], idx1, "v1_0"))
+                v1_scales = gather_scales(plane1, idx1, "v1_scales")
+                joined_tile = ring.tile([P, 2, PICK], F32, name="joined23", tag="plane1", align_bytes=64)
+            if s == 4:
+                qa[(0, 0)] = quantize_weight(raw_a[(0, 0)], "wa00")
+                qa[(1, 0)] = quantize_weight(raw_a[(1, 0)], "wa10")
+                v1.append(gather_words(words1[1], idx1, "v1_1"))
+                two_caps = ring.tile([P, 4], F32, name="two_caps_late", tag="raw0")
+                nc.scalar.mul(two_caps[:], caps[:, 4:8], 2.0)
+                joined_tile = ring.tile([P, 4, PICK], F32, name="joined4567", tag="words2")
+            passes = [(wd_codes[:, 2 * P * s : 2 * P * (s + 1)].bitcast(FP4X4), wd_scale_plane[:, P * s : P * (s + 1)], v3, v3_scales)]
+            window = first_stage((2 * s) % 8, passes, ACT.Identity, -1.0, two_caps[:, s % 4 : s % 4 + 1])
+            joined.append(pick_and(ALU.subtract, joined_tile[:, s % (2 if s < 4 else 4), :], window, p3[:], picked_b[s]))
+
+        qa[(0, 1)] = quantize_weight(raw_a[(0, 1)], "wa01")
+        qa[(1, 1)] = quantize_weight(raw_a[(1, 1)], "wa11")
         cap_for_a = ring.tile([P, SLICES], F32, name="cap_for_a", tag="raw3")
         nc.scalar.copy(cap_for_a[:], caps)
-        two_caps = keep.tile([P, SLICES], F32, name="two_caps")
-        nc.scalar.mul(two_caps[:], caps, 2.0)
-        wd_scale_plane = keep.tile([P, H], U8, name="wd_scale_plane", align_bytes=64)
-        nc.vector.tensor_copy(
-            wd_scale_plane[:].rearrange("p (g t m) -> p g t m", g=2, t=4),
-            wd_plane[:].rearrange("p (g m t) -> p g t m", g=2, t=4),
-        )
-        joined = []
-        early_a = ring.tile([P, 4, PICK], F32, name="early_a")
-        for s in range(SLICES):
-            if s == 4:
-                v3 = gather_words(words3, idx3, "v3")
-                late_a = ring.tile([P, 4, PICK], F32, name="late_a", tag="words23")
-            passes = [weight_pass(qa[(g, s // 4)], s) + (v1[g], v1_scales[8 + 4 * g : P, :]) for g in range(2)]
-            window = first_stage((2 * s) % 8, passes, ACT.Relu, -1.0, cap_for_a[:, s : s + 1])
-            joined.append(pick_and(ALU.add, (early_a if s < 4 else late_a)[:, s % 4, :], window, p1[:], picked_b[s]))
-
         half = PICK // 2
-        windows_d = []
+        windows_a = []
         z_first = ring.tile([P, 4, PICK], F32, name="z_first")
         z_left = ring.tile([P, 4, half], F32, name="z_left")
         for s in range(SLICES):
-            passes = [(wd_codes[:, 2 * P * s : 2 * P * (s + 1)].bitcast(FP4X4), wd_scale_plane[:, P * s : P * (s + 1)], v3, v3_scales)]
-            window = first_stage((2 * s) % 8, passes, ACT.Identity, -1.0, two_caps[:, s : s + 1])
-            windows_d.append(window)
+            passes = [weight_pass(qa[(g, s // 4)], s) + (v1[g], v1_scales[8 + 4 * g : P, :]) for g in range(2)]
+            window = first_stage((2 * s) % 8, passes, ACT.Relu, -1.0, cap_for_a[:, s : s + 1])
+            windows_a.append(window)
             if s < 4:
-                pick_and(ALU.subtract, z_first[:, s, :], window, p3[:], joined[s])
+                pick_and(ALU.subtract, z_first[:, s, :], window, p1[:], joined[s])
             else:
-                pick_and(ALU.subtract, z_left[:, s - 4, :], window, p3[:, 0:16], joined[s][:, 0:half])
+                pick_and(ALU.subtract, z_left[:, s - 4, :], window, p1[:, 0:16], joined[s][:, 0:half])
 
         z_codes = [keep.tile([P, PICK], U32, name="z_codes%d" % g, align_bytes=64) for g in range(2)]
         z_scales = [keep.tile([P, PICK], U8, name="z_scales%d" % g, align_bytes=64) for g in range(2)]
 
-        def quantize_z(rows, g, first, copy, tag):
+        def quantize_z(rows, g, first, on_scalar, tag):
             width = rows.shape[2]
             woven = ring.tile([P, width, 4], BF16, name="woven", tag=tag, align_bytes=64)
-            copy(
-                woven[:].rearrange("p (c i) t -> p c t i", i=4),
-                rows.rearrange("p t (c i) -> p c t i", i=4),
-            )
+            dst = woven[:].rearrange("p (c i) t -> p c t i", i=4)
+            src = rows.rearrange("p t (c i) -> p c t i", i=4)
+            if on_scalar:
+                nc.scalar.activation(dst, src, ACT.Copy, scale=-1.0)
+            else:
+                nc.vector.tensor_scalar(dst, src, -1.0, None, ALU.mult)
             cols = slice(first, first + width)
             nc.vector.quantize_mx(
                 out=z_codes[g][:, cols].bitcast(FP8X4), scales=z_scales[g][:, cols],
                 in_=woven[:].rearrange("p j t -> p (j t)"),
             )
 
-        quantize_z(z_first[:, :, 0:half], 0, 0, nc.scalar.copy, "woven0")
-        z_right = ring.tile([P, 4, half], F32, name="z_right", tag="woven0", align_bytes=64)
-        for s in range(4, SLICES):
-            pick_and(ALU.subtract, z_right[:, s - 4, :], windows_d[s], p3[:, 16:32], joined[s][:, half:PICK])
-        quantize_z(z_first[:, :, half:PICK], 0, half, nc.scalar.copy, "woven1")
+        quantize_z(z_first[:, :, 0:half], 0, 0, True, "woven0")
+        quantize_z(z_first[:, :, half:PICK], 0, half, True, "woven1")
         ys = [bank(jt) for jt in range(JT)]
 
         def last_product(g, jt):
@@ -263,13 +272,17 @@ def tile_list_claim_rating_features_kernel(
         for jt in range(JT):
             last_product(0, jt)
         for jt in range(JT):
+            if jt == 2:
+                z_right = ring.tile([P, 4, half], F32, name="z_right", tag="woven_last1", align_bytes=64)
+                for s in range(4, SLICES):
+                    pick_and(ALU.subtract, z_right[:, s - 4, :], windows_a[s], p1[:, 16:32], joined[s][:, half:PICK])
             rows = (z_left if jt < 2 else z_right)[:, :, P * (jt % 2) : P * (jt % 2 + 1)]
-            quantize_z(rows, 1, P * jt, nc.vector.tensor_copy if jt == 3 else nc.scalar.copy, "woven_last%d" % jt)
+            quantize_z(rows, 1, P * jt, jt == 0, "woven_last%d" % jt)
             last_product(1, jt)
 
-        sizes = ring.tile([P, JT, BANK], F32, name="sizes", tag="words11")
+        sizes = ring.tile([P, JT, BANK], F32, name="sizes", tag="words10")
         roots = ring.tile([P, JT, BANK], F32, name="roots", tag="raw1")
-        parts = ring.tile([P, JT, BANK], F32, name="parts", tag="raw0")
+        parts = ring.tile([P, JT, BANK], F32, name="parts", tag="words3")
         results = ring.tile([P, JT, BANK], F32, name="results", tag="raw2")
         for jt in range(JT):
             cols = slice(P * jt, P * (jt + 1))

from contextlib import ExitStack

import concourse.mybir as mybir

K, M, H, N, T, S, PICK = 1024, 512, 1024, 512, 4096, 1024, 512
FLOPS = 2 * (K * H * S + 2 * M * H * S + H * N * PICK)

F32 = mybir.dt.float32
BF16 = mybir.dt.bfloat16
I32 = mybir.dt.int32
U32 = mybir.dt.uint32
U16 = mybir.dt.uint16
U8 = mybir.dt.uint8
FP8X4 = mybir.dt.float8_e4m3fn_x4
FP4X4 = mybir.dt.float4_e2m1fn_x4
ACT = mybir.ActivationFunctionType
ALU = mybir.AluOpType

P = 128
BANK = 512
SLICES = H // P
JT = PICK // P


def tile_list_claim_rating_features_kernel(
    tc, tab_words, tab_scales, tab2_words, tab2_scales, tab3_words, tab3_scales,
    offs, offs2, offs3, pos1, pos2, pos3, wa, wb, wd_words, wd_scales, cap,
    w4_words, w4_scales, out,
):
    nc = tc.nc
    with ExitStack() as ctx:
        lists = ctx.enter_context(tc.tile_pool(name="lists", bufs=1))
        keep = ctx.enter_context(tc.tile_pool(name="keep", bufs=1))
        ring = ctx.enter_context(tc.tile_pool(name="ring", bufs=1))
        psum = ctx.enter_context(tc.psum_pool(name="psum", bufs=1))

        def bank(i):
            return psum.tile([P, BANK], F32, name="bank%d" % i)

        def load_list(src, name):
            t = lists.tile([P, src.shape[1]], U16, name=name)
            nc.sync.dma_start(t[:], src)
            return t

        def load_words(src, tag):
            t = ring.tile([P, T], I32, name="table_words", tag=tag)
            nc.sync.dma_start(t[:], src.rearrange("p t i -> p (t i)").bitcast(I32))
            return t

        def zeroed_plane(width, name):
            t = ring.tile([P, width], U8, name=name, tag=name, align_bytes=64)
            nc.vector.memset(t[:].bitcast(I32), 0)
            return t

        def load_scale_rows(queue, plane, first_row, src):
            rows = 4 * src.shape[0]
            for q in range(4):
                lo = 32 * q + first_row
                queue.dma_start(
                    plane[lo : lo + rows, :].bitcast(I32),
                    src[:, 4 * q : 4 * q + 4, :].bitcast(I32),
                )

        def load_weight(w, g, half, tag):
            t = ring.tile([P, 4, BANK], F32, name="raw_weight", tag=tag)
            rows = w[512 * g : 512 * (g + 1), BANK * half : BANK * (half + 1)]
            nc.sync.dma_start(t[:], rows.rearrange("(p t) c -> p t c", t=4))
            return t

        warm = keep.tile([P, 2], F32, name="warm")
        nc.gpsimd.memset(warm[:], 1.0)
        nc.scalar.activation(warm[:, 1:2], warm[:, 0:1], ACT.Abs_reciprocal_sqrt)

        plane2 = zeroed_plane(T, "plane2")
        wd_plane = zeroed_plane(H, "wd_plane")
        plane3 = zeroed_plane(T, "plane3")
        plane1 = zeroed_plane(T, "plane1")
        w4_plane = zeroed_plane(2 * N, "w4_plane")

        raw_b = [load_weight(wb, 0, 0, "raw0")]
        load_scale_rows(nc.sync, plane2, 4, tab2_scales)
        idx2 = load_list(offs2, "idx2")
        wd_raw = keep.tile([P, 2 * H], U8, name="wd_raw", align_bytes=64)
        nc.sync.dma_start(wd_raw[:].bitcast(I32), wd_words[0].bitcast(I32))
        words2 = load_words(tab2_words[0], "words2")
        cap_col = keep.tile([P, 2, 4], F32, name="cap_col")
        nc.sync.dma_start(cap_col[:], cap.rearrange("(g p t) -> p g t", g=2, t=4))
        p2 = load_list(pos2, "p2")
        load_scale_rows(nc.sync, wd_plane, 0, wd_scales)
        raw_b.append(load_weight(wb, 0, 1, "raw1"))
        words3 = load_words(tab3_words[0], "words3")
        idx3 = load_list(offs3, "idx3")
        load_scale_rows(nc.sync, plane3, 0, tab3_scales)
        p3 = load_list(pos3, "p3")
        words1 = [load_words(tab_words[0], "words10")]
        idx1 = load_list(offs, "idx1")
        load_scale_rows(nc.sync, plane1, 8, tab_scales)
        raw_a = {(0, 0): load_weight(wa, 0, 0, "raw2")}
        raw_a[(1, 0)] = load_weight(wa, 1, 0, "raw0")
        caps = cap_col[:].rearrange("p g t -> p (g t)")

        def gather_scales(plane, idx, name):
            t = keep.tile([P, S], U8, name=name, align_bytes=64)
            nc.vector.tensor_copy(t[:], plane[:].indirect(idx[:]))
            return t

        def gather_words(words, idx, name, pieces=1):
            t = keep.tile([P, S], U32, name=name, align_bytes=64)
            width = S // pieces
            for i in range(pieces):
                nc.vector.tensor_copy(
                    t[:, width * i : width * (i + 1)],
                    words[:].bitcast(U32).indirect(idx[:, width // 16 * i : width // 16 * (i + 1)]),
                )
            return t

        def quantize_weight(raw, name):
            grouped = ring.tile([P, BANK, 4], BF16, name="grouped", bufs=3, align_bytes=64)
            nc.scalar.copy(
                grouped[:].rearrange("p (t m) j -> p m j t", t=4),
                raw[:].rearrange("p j (m t) -> p m j t", t=4),
            )
            codes = keep.tile([P, BANK], U32, name=name + "_codes", align_bytes=64)
            scales = keep.tile([P, BANK], U8, name=name + "_scales", align_bytes=64)
            nc.vector.quantize_mx(
                out=codes[:].bitcast(FP8X4), scales=scales[:],
                in_=grouped[:].rearrange("p c t -> p (c t)"),
            )
            return codes, scales

        def first_stage(first_bank, passes, func, scale, bias, tag=None):
            if tag is None:
                window = ring.tile([P, S], F32, name="window", bufs=8)
            else:
                window = ring.tile([P, S], F32, name="window", tag=tag)
            for h in range(2):
                cols = slice(BANK * h, BANK * (h + 1))
                acc = bank(first_bank + h)
                for g, (lhs, lhs_scale, rhs, rhs_scale) in enumerate(passes):
                    nc.tensor.matmul_mx(
                        out=acc[:], lhsT=lhs, lhsT_scale=lhs_scale,
                        rhs=rhs[:, cols].bitcast(FP8X4), rhs_scale=rhs_scale[:, cols],
                        start=(g == 0), stop=(g == len(passes) - 1),
                    )
                nc.scalar.activation(window[:, cols], acc[:], func, bias=bias, scale=scale)
            return window

        def pick(picked, window, pos):
            nc.vector.tensor_copy(picked, window[:].indirect(pos))
            return picked

        def pick_and(op, result, window, pos, other):
            nc.vector.tensor_tensor(result, window[:].indirect(pos), other, op)
            return result

        def weight_pass(q, s):
            codes, scales = q
            cols = slice(P * (s % 4), P * (s % 4 + 1))
            return codes[:, cols].bitcast(FP8X4), scales[:, cols]

        v2_scales = gather_scales(plane2, idx2, "v2_scales")
        qb = [quantize_weight(raw_b[0], "wb0")]
        v2 = gather_words(words2, idx2, "v2", 2)
        wd_codes = keep.tile([P, 2 * H], U8, name="wd_codes", align_bytes=64)
        nc.vector.tensor_copy(
            wd_codes[:].rearrange("p (g t m e) -> p g t m e", g=2, t=4, e=2),
            wd_raw[:].rearrange("p (g m t e) -> p g t m e", g=2, t=4, e=2),
        )
        wd_scale_plane = keep.tile([P, H], U8, name="wd_scale_plane", align_bytes=64)
        nc.vector.tensor_copy(
            wd_scale_plane[:].rearrange("p (g t m) -> p g t m", g=2, t=4),
            wd_plane[:].rearrange("p (g m t) -> p g t m", g=2, t=4),
        )
        picked_b = []
        early_b = ring.tile([P, 4, PICK], F32, name="early_b")
        for s in range(SLICES):
            if s == 2:
                qb.append(quantize_weight(raw_b[1], "wb1"))
            if s == 4:
                v3 = gather_words(words3, idx3, "v3")
                v3_scales = gather_scales(plane3, idx3, "v3_scales")
                late_b = ring.tile([P, 4, PICK], F32, name="late_b", tag="plane3", align_bytes=64)
            passes = [weight_pass(qb[s // 4], s) + (v2, v2_scales[4:P, :])]
            window = first_stage((2 * s) % 8, passes, ACT.Relu, -1.0, caps[:, s : s + 1], "raw1" if s == 2 else None)
            picked_b.append(pick((early_b if s < 4 else late_b)[:, s % 4, :], window, p2[:]))

        words1.append(load_words(tab_words[1], "words2"))
        p1 = load_list(pos1, "p1")
        raw_a[(0, 1)] = load_weight(wa, 0, 1, "raw1")
        raw_a[(1, 1)] = load_weight(wa, 1, 1, "raw3")
        w4_codes = keep.tile([P, 2, 2 * N], U8, name="w4_codes", align_bytes=64)
        nc.sync.dma_start(w4_codes[:].bitcast(I32), w4_words.rearrange("g p c -> p g c").bitcast(I32))
        for q in range(4):
            nc.sync.dma_start(
                w4_plane[32 * q : 32 * q + 4, :].bitcast(I32).rearrange("r (g c) -> r g c", g=2),
                w4_scales[:, 4 * q : 4 * q + 4, :].bitcast(I32).rearrange("g r c -> r g c"),
            )

        joined = []
        qa = {}
        v1 = []
        for s in range(SLICES):
            if s == 0:
                two_caps = keep.tile([P, 4], F32, name="two_caps")
                nc.scalar.mul(two_caps[:], caps[:, 0:4], 2.0)
                joined_tile = ring.tile([P, 2, PICK], F32, name="joined01")
            if s == 2:
                v1.append(gather_words(words1[0], idx1, "v1_0"))
                v1_scales = gather_scales(plane1, idx1, "v1_scales")
                joined_tile = ring.tile([P, 2, PICK], F32, name="joined23", tag="plane1", align_bytes=64)
            if s == 4:
                qa[(0, 0)] = quantize_weight(raw_a[(0, 0)], "wa00")
                qa[(1, 0)] = quantize_weight(raw_a[(1, 0)], "wa10")
                v1.append(gather_words(words1[1], idx1, "v1_1"))
                two_caps = ring.tile([P, 4], F32, name="two_caps_late", tag="raw0")
                nc.scalar.mul(two_caps[:], caps[:, 4:8], 2.0)
                joined_tile = ring.tile([P, 4, PICK], F32, name="joined4567", tag="words2")
            passes = [(wd_codes[:, 2 * P * s : 2 * P * (s + 1)].bitcast(FP4X4), wd_scale_plane[:, P * s : P * (s + 1)], v3, v3_scales)]
            window = first_stage((2 * s) % 8, passes, ACT.Identity, -1.0, two_caps[:, s % 4 : s % 4 + 1])
            joined.append(pick_and(ALU.subtract, joined_tile[:, s % (2 if s < 4 else 4), :], window, p3[:], picked_b[s]))

        qa[(0, 1)] = quantize_weight(raw_a[(0, 1)], "wa01")
        qa[(1, 1)] = quantize_weight(raw_a[(1, 1)], "wa11")
        cap_for_a = ring.tile([P, SLICES], F32, name="cap_for_a", tag="raw3")
        nc.scalar.copy(cap_for_a[:], caps)
        half = PICK // 2
        windows_a = []
        z_first = ring.tile([P, 4, PICK], F32, name="z_first")
        z_left = ring.tile([P, 4, half], F32, name="z_left")
        for s in range(SLICES):
            passes = [weight_pass(qa[(g, s // 4)], s) + (v1[g], v1_scales[8 + 4 * g : P, :]) for g in range(2)]
            window = first_stage((2 * s) % 8, passes, ACT.Relu, -1.0, cap_for_a[:, s : s + 1])
            windows_a.append(window)
            if s < 4:
                pick_and(ALU.subtract, z_first[:, s, :], window, p1[:], joined[s])
            else:
                pick_and(ALU.subtract, z_left[:, s - 4, :], window, p1[:, 0:16], joined[s][:, 0:half])

        z_codes = [keep.tile([P, PICK], U32, name="z_codes%d" % g, align_bytes=64) for g in range(2)]
        z_scales = [keep.tile([P, PICK], U8, name="z_scales%d" % g, align_bytes=64) for g in range(2)]

        def quantize_z(rows, g, first, on_scalar, tag):
            width = rows.shape[2]
            woven = ring.tile([P, width, 4], BF16, name="woven", tag=tag, align_bytes=64)
            dst = woven[:].rearrange("p (c i) t -> p c t i", i=4)
            src = rows.rearrange("p t (c i) -> p c t i", i=4)
            if on_scalar:
                nc.scalar.activation(dst, src, ACT.Copy, scale=-1.0)
            else:
                nc.vector.tensor_scalar(dst, src, -1.0, None, ALU.mult)
            cols = slice(first, first + width)
            nc.vector.quantize_mx(
                out=z_codes[g][:, cols].bitcast(FP8X4), scales=z_scales[g][:, cols],
                in_=woven[:].rearrange("p j t -> p (j t)"),
            )

        quantize_z(z_first[:, :, 0:half], 0, 0, True, "woven0")
        quantize_z(z_first[:, :, half:PICK], 0, half, True, "woven1")
        ys = [bank(jt) for jt in range(JT)]

        def last_product(g, jt):
            cols = slice(P * jt, P * (jt + 1))
            for nt in range(N // P):
                nc.tensor.matmul_mx(
                    out=ys[jt][:, P * nt : P * (nt + 1)],
                    lhsT=w4_codes[:, g, 2 * P * nt : 2 * P * (nt + 1)].bitcast(FP4X4),
                    lhsT_scale=w4_plane[:, N * g + P * nt : N * g + P * (nt + 1)],
                    rhs=z_codes[g][:, cols].bitcast(FP8X4), rhs_scale=z_scales[g][:, cols],
                    start=(g == 0 and nt == 0), stop=(g == 1 and nt == N // P - 1),
                )

        for jt in range(JT):
            last_product(0, jt)
        for jt in range(JT):
            if jt == 2:
                z_right = ring.tile([P, 4, half], F32, name="z_right", tag="woven_last1", align_bytes=64)
                for s in range(4, SLICES):
                    pick_and(ALU.subtract, z_right[:, s - 4, :], windows_a[s], p1[:, 16:32], joined[s][:, half:PICK])
            rows = (z_left if jt < 2 else z_right)[:, :, P * (jt % 2) : P * (jt % 2 + 1)]
            quantize_z(rows, 1, P * jt, jt == 0, "woven_last%d" % jt)
            last_product(1, jt)

        sizes = ring.tile([P, JT, BANK], F32, name="sizes", tag="words10")
        roots = ring.tile([P, JT, BANK], F32, name="roots", tag="raw1")
        parts = ring.tile([P, JT, BANK], F32, name="parts", tag="words3")
        results = ring.tile([P, JT, BANK], F32, name="results", tag="raw2")
        for jt in range(JT):
            cols = slice(P * jt, P * (jt + 1))
            y = ys[jt]
            nc.scalar.activation(sizes[:, jt, :], y[:], ACT.Abs)
            nc.scalar.activation(roots[:, jt, :], sizes[:, jt, :], ACT.Abs_reciprocal_sqrt, bias=1.0)
            nc.vector.tensor_tensor(parts[:, jt, :], y[:], roots[:, jt, :], ALU.mult)
            nc.vector.tensor_tensor(results[:, jt, :], parts[:, jt, :], roots[:, jt, :], ALU.mult)
            nc.sync.dma_start(out.rearrange("(n p) j -> p n j", p=P)[:, :, cols], results[:, jt, :].rearrange("p (n j) -> p n j", j=P))
